import numpy as np
import ml_dtypes


def mxq(x, axis, fmt="e4m3"):
    dtype, down = {"e4m3": (ml_dtypes.float8_e4m3fn, 7), "e5m2": (ml_dtypes.float8_e5m2, 14)}[fmt]
    v = np.moveaxis(np.asarray(x, np.float32).astype(ml_dtypes.bfloat16).astype(np.float64), axis, -1)
    blocks = v.reshape(v.shape[:-1] + (-1, 32))
    amax = np.abs(blocks).max(-1, keepdims=True)
    byte = np.maximum(np.where(amax > 0, np.frexp(amax)[1] - 1 + 127, 0) - down, 1)
    scale = np.exp2(byte - 127.0)
    codes = (blocks / scale).astype(np.float32).astype(dtype).astype(np.float64)
    return np.moveaxis((codes * scale).reshape(v.shape), -1, axis)


WIDE = False


def mx_kscale(k):
    if not WIDE:
        return np.ones(k)
    levels = np.array([10, -10, 5, -5, 0])
    if k % 512:
        return np.exp2(np.random.permutation(np.resize(levels, k // 32))).repeat(32)
    a = np.empty((k // 512, 16))
    for p in range(k // 512):
        a[p, :8] = np.random.permutation(np.resize(levels, 8))
        for g in range(8):
            far = levels[np.abs(levels - a[p, g]) >= 10]
            a[p, g + 8] = far[np.random.randint(len(far))]
    return np.exp2(a.ravel()).repeat(32)


def f64(x):
    return np.asarray(x).astype(np.float64)


def striped(idx):
    return np.tile(idx.reshape(-1, 16).T, (8, 1)).astype(np.uint16)


def unstriped(offs):
    return offs[:16].T.reshape(-1).astype(np.int64)


def striped8(idx):
    return np.concatenate([x.reshape(-1, 16).T for x in idx]).astype(np.uint16)


def runs(offs, k):
    lists = np.stack([offs[16 * r : 16 * r + 16].T.reshape(-1) for r in range(8)]).astype(np.int64)
    return lists[np.arange(k) % 512 // 64]


def pack_weight(w):
    k, n = w.shape
    w = f64(np.asarray(w, np.float32).astype(ml_dtypes.bfloat16)).reshape(k // 32, 32, n)
    amax = np.abs(w).max(1)
    byte = np.clip(np.where(amax > 0, np.frexp(amax)[1] - 1 + 127 - 7, 1), 1, 254)
    scaled = (w * np.exp2(127.0 - byte)[:, None, :]).reshape(k, n).astype(np.float32)
    words = np.ascontiguousarray(scaled.reshape(k // 512, 128, 4, n).transpose(0, 1, 3, 2)).astype(ml_dtypes.float8_e4m3fn).view(np.uint8)
    return words, np.ascontiguousarray(byte.astype(np.uint8).reshape(k // 512, 16, n))


def unpack_weight(words, scales):
    g, p, n, _ = words.shape
    vals = np.ascontiguousarray(words).view(ml_dtypes.float8_e4m3fn).astype(np.float64) * np.repeat(np.exp2(scales.astype(np.float64) - 127.0), 8, axis=1)[..., None]
    return vals.transpose(0, 1, 3, 2).reshape(g * 512, n)


def sigmoid(v):
    return 1.0 / (1.0 + np.exp(-np.maximum(v, -700.0)))


K, T, S, N, G, H, W = 512, 1024, 512, 512, 2048, 512, 256


def setup_inputs():
    n = np.random.standard_normal
    s = mx_kscale(K)[:, None]
    u = mx_kscale(S)
    packed_xT = pack_weight(n((K, T)) * s)
    packed_dT = pack_weight(n((K, G)) / s)
    perm = np.stack([np.random.permutation(S) for _ in range(8)])
    return {
        "x_words": packed_xT[0],
        "x_scales": packed_xT[1],
        "d_words": packed_dT[0],
        "d_scales": packed_dT[1],
        "gn": (np.random.uniform(0.5, 1.5, (H, 1)) * u[:, None]).astype(np.float32),
        "gm": (np.random.uniform(0.5, 1.5, (H, 1)) * u[:, None]).astype(np.float32),
        "w1": (n((H, N)) / np.sqrt(2 * H) / u[:, None]).astype(np.float32),
        "w2": (n((H, N)) / np.sqrt(2 * H) / u[:, None]).astype(np.float32),
        "offs": striped(np.random.permutation(T)[:S]),
        "k1": striped8(np.random.randint(0, G, (8, H))),
        "two": striped(np.random.permutation(T)[:S]),
        "n1": striped8(perm[:, :W]),
        "n2": striped8(perm[:, W:]),
        "n3": striped8(np.stack([np.random.permutation(S) for _ in range(8)])),
        "n4": striped8(np.stack([np.random.permutation(S) for _ in range(8)])),
        "n5": striped(np.random.randint(0, S, G)),
    }


def reference(x_words, x_scales, d_words, d_scales, gn, gm, w1, w2, offs, k1, two, n1, n2, n3, n4, n5):
    d_k1 = unpack_weight(d_words, d_scales)[np.arange(K)[:, None], runs(k1, K)]
    xq = unpack_weight(x_words, x_scales)[:, unstriped(offs)]
    a = 0.0625 * (d_k1.T @ xq)
    pb = a[np.arange(H)[:, None], runs(n2, H)]
    pa = a[np.arange(H)[:, None], runs(n1, H)]
    rb = pb * sigmoid(pb - pa)
    ra = pa * sigmoid(pa - pb)
    ds = np.zeros((H, S))
    ds[np.arange(H)[:, None], runs(n1, H)] = ra
    dt = ds.copy()
    dt[np.arange(H)[:, None], runs(n2, H)] = rb
    z = f64(gn) * dt
    x_two = unpack_weight(x_words, x_scales)[:, unstriped(two)]
    b = 0.0625 * (d_k1.T @ x_two)
    z2 = f64(gm) * (np.minimum(np.maximum(b, b[np.arange(H)[:, None], runs(n3, H)]), b[np.arange(H)[:, None], runs(n4, H)]))
    h = mxq(f64(w1), 0, "e4m3").T @ mxq(z, 0, "e4m3") + mxq(f64(w2), 0, "e4m3").T @ mxq(z2, 0, "e4m3")
    mb = h[:, unstriped(n5)]
    mx = mb.reshape(N, S, 4).max(axis=2)
    mn = mb.reshape(N, S, 4).min(axis=2)
    return mx * np.tanh(h - mn)

@@ -1,0 +1,287 @@
+from contextlib import ExitStack
+
+import concourse.mybir as mybir
+
+K, T, S, N, G, H, W = 512, 1024, 512, 512, 2048, 512, 256
+FLOPS = 4 * 2 * 512 * 512 * 512
+
+F32 = mybir.dt.float32
+BF16 = mybir.dt.bfloat16
+I32 = mybir.dt.int32
+U32 = mybir.dt.uint32
+U16 = mybir.dt.uint16
+U8 = mybir.dt.uint8
+FP8X4 = mybir.dt.float8_e4m3fn_x4
+ALU = mybir.AluOpType
+ACT = mybir.ActivationFunctionType
+
+P = 128
+PACK = 4
+SPARE = 16
+CHUNKS = ((0, 256), (256, 128), (384, 128))
+PIECE = 512
+STEPS = ((256, 256), (256, 256), (256, 256), (256, 128, 128))
+
+
+def walk_out(ap):
+    return ap.rearrange("p (c i t) -> p c t i", i=4, t=PACK)
+
+
+def walk_in(ap):
+    return ap.rearrange("p t (c i) -> p c t i", i=4)
+
+
+def tile_picked_kjduelminmxgtan_none_p_kernel(
+    tc, x_words, x_scales, d_words, d_scales, gn, gm, w1, w2, offs, k1, two, n1, n2, n3, n4, n5, out
+):
+    nc = tc.nc
+    with ExitStack() as ctx:
+        keep = ctx.enter_context(tc.tile_pool(name="keep", bufs=1))
+        ring = ctx.enter_context(tc.tile_pool(name="ring", bufs=2))
+        psum = ctx.enter_context(tc.psum_pool(name="psum", bufs=1))
+
+        def load_list(src, name):
+            lst = keep.tile(list(src.shape), U16, name=name)
+            nc.sync.dma_start(lst[:], src)
+            return lst
+
+        def load_scales(src, width, name, tag):
+            rows = keep.tile([P, width], U8, name=name, tag=tag)
+            nc.sync.dma_start(rows[:].bitcast(I32), src[0].bitcast(I32).unsqueeze(1).to_broadcast([16, 8, width // 4]))
+            return rows
+
+        def load_words(src, width, name):
+            words = keep.tile([P, width], U32, name=name)
+            nc.sync.dma_start(words[:].bitcast(I32), src[0].rearrange("p n t -> p (n t)").bitcast(I32))
+            return words
+
+        def load_rows(src, name, tag, queue=nc.sync):
+            raw = keep.tile([P, PACK, src.shape[1]], F32, name=name, tag=tag)
+            queue.dma_start(raw[:], src.rearrange("(p t) n -> p t n", t=PACK))
+            return raw
+
+        def quantize(grouped, width, name):
+            codes = keep.tile([P, width], U32, name=name + "_codes", align_bytes=64)
+            scales = keep.tile([P, width], U8, name=name + "_scales", align_bytes=64)
+            nc.vector.quantize_mx(out=codes[:].bitcast(FP8X4), scales=scales[:], in_=grouped[:])
+            return codes, scales
+
+        placed = keep.tile([P, 3 * S], U8, name="placed", align_bytes=64)
+        nc.gpsimd.memset(placed[:].bitcast(I32), 0)
+        h_rows = [keep.tile([P, S + SPARE], F32, name="h_rows%d" % m) for m in range(4)]
+        for m in range(4):
+            nc.gpsimd.memset(h_rows[m][:, S:], 0.0)
+
+        gm_t = load_rows(gm, "gm_t", "gm_t")
+        ds_rows = load_scales(d_scales, G, "ds_rows", "ds_rows")
+        k1_l = load_list(k1, "k1_l")
+        xs_rows = load_scales(x_scales, T, "xs_rows", "xs_rows")
+        offs_l = load_list(offs, "offs_l")
+        two_l = load_list(two, "two_l")
+        xw = load_words(x_words, T, "xw")
+        w2_raw = [keep.tile([P, N], F32, name="w2_raw%d" % t) for t in range(PACK)]
+        for t in range(PACK):
+            nc.sync.dma_start(w2_raw[t][:], w2.rearrange("(p t) n -> p t n", t=PACK)[:, t, :])
+        dw = load_words(d_words, G, "dw")
+        n1_l = load_list(n1, "n1_l")
+        n2_l = load_list(n2, "n2_l")
+
+        picked = keep.tile([P, 3 * S], U8, name="picked", tag="picked_then_w1")
+        nc.vector.tensor_copy(picked[:, 0:S], ds_rows[:].indirect(k1_l[:]))
+        nc.vector.tensor_copy(picked[:, S : 2 * S], xs_rows[:].indirect(offs_l[:]))
+        nc.vector.tensor_copy(picked[:, 2 * S : 3 * S], xs_rows[:].indirect(two_l[:]))
+        dealt = keep.tile([P, 3 * S], U8, name="dealt")
+        nc.vector.tensor_copy(
+            dealt[:, 0:S].rearrange("p (t m) -> p t m", t=PACK),
+            picked[:, 0:S].rearrange("p (m t) -> p t m", t=PACK),
+        )
+        nc.vector.tensor_copy(dealt[:, S:].bitcast(I32), picked[:, S:].bitcast(I32))
+        for r in range(4):
+            nc.sync.dma_start(placed[r:P:32, :].bitcast(I32), dealt[8 * r : P : 32, :].bitcast(I32))
+        w1_raw = load_rows(w1, "w1_raw", "picked_then_w1")
+        gn_t = load_rows(gn, "gn_t", "gn_t")
+        n3_l = load_list(n3, "n3_l")
+        n4_l = load_list(n4, "n4_l")
+        n5_l = load_list(n5, "n5_l")
+
+        gm_sign = keep.tile([P, PACK], F32, name="gm_sign")
+        gm_size = keep.tile([P, PACK], F32, name="gm_size")
+        nc.scalar.activation(gm_sign[:], gm_t[:, :, 0], ACT.Sign)
+        nc.scalar.activation(gm_size[:], gm_t[:, :, 0], ACT.Abs, scale=0.0625)
+        w2_signed = keep.tile([P, PACK, N], BF16, name="w2_signed")
+        for t in range(PACK):
+            nc.scalar.activation(w2_signed[:, t, :], w2_raw[t][:], ACT.Copy, scale=gm_sign[:, t : t + 1])
+        w2_grouped = keep.tile([P, PACK * N], BF16, name="w2_grouped", align_bytes=64)
+        nc.scalar.copy(walk_out(w2_grouped[:]), walk_in(w2_signed[:]))
+
+        xa = keep.tile([P, S], U32, name="xa", align_bytes=64)
+        keys = keep.tile([P, H], U32, name="keys", tag="keys_then_xb", align_bytes=64)
+        nc.vector.tensor_copy(xa[:], xw[:].indirect(offs_l[:]))
+        nc.vector.tensor_copy(keys[:], dw[:].indirect(k1_l[:]))
+        keys_dealt = keep.tile([P, H], U32, name="keys_dealt", align_bytes=64)
+        nc.vector.tensor_copy(
+            keys_dealt[:].bitcast(I32).rearrange("p (t c i) -> p c t i", t=PACK, i=4),
+            keys[:].bitcast(I32).rearrange("p (c i t) -> p c t i", t=PACK, i=4),
+        )
+        xb = keep.tile([P, S], U32, name="xb", tag="keys_then_xb", align_bytes=64)
+        nc.vector.tensor_copy(xb[:], xw[:].indirect(two_l[:]))
+
+        def scores(t, words, scale_cols, bank):
+            acc = psum.tile([P, S], F32, name="acc_" + bank, tag=bank)
+            cols = slice(P * t, P * (t + 1))
+            nc.tensor.matmul_mx(
+                out=acc[:],
+                lhsT=keys_dealt[:, cols].bitcast(FP8X4),
+                lhsT_scale=placed[:, cols],
+                rhs=words[:].bitcast(FP8X4),
+                rhs_scale=placed[:, scale_cols],
+                start=True,
+                stop=True,
+            )
+            return acc
+
+        a_acc = [scores(t, xa, slice(S, 2 * S), "bank%d" % t) for t in range(PACK)]
+        b_acc = [scores(t, xb, slice(2 * S, 3 * S), "bank%d" % (PACK + t)) for t in range(PACK)]
+
+        w2_q = quantize(w2_grouped, N, "w2")
+        w1_grouped = keep.tile([P, PACK * N], BF16, name="w1_grouped", align_bytes=64)
+
+        z_rows = keep.tile([P, PACK, S], BF16, name="z_rows")
+        larger = keep.tile([P, PACK, S], F32, name="larger")
+        a_rows = [keep.tile([P, S], F32, name="a_rows%d" % t) for t in range(PACK)]
+        b_rows = [keep.tile([P, S], F32, name="b_rows%d" % t) for t in range(PACK)]
+        dt_rows = [keep.tile([P, S], F32, name="dt_rows%d" % t) for t in range(PACK)]
+        pair = [keep.tile([P, 2, W], F32, name="pair%d" % t) for t in range(PACK)]
+        gate = [keep.tile([P, 2, W], F32, name="gate%d" % t) for t in range(PACK)]
+        diff = [keep.tile([P, W], F32, name="diff%d" % t) for t in range(PACK)]
+
+        def leave_a(t):
+            nc.scalar.activation(a_rows[t][:], a_acc[t][:], ACT.Copy, scale=0.0625)
+
+        pair_lists = (n1_l, n2_l)
+
+        def fetch(t, side):
+            nc.scalar.activation(pair[t][:, side, :], a_rows[t][:].indirect(pair_lists[side][:]), ACT.Copy)
+            if side == 1:
+                nc.vector.tensor_tensor(diff[t][:], pair[t][:, 0, :], pair[t][:, 1, :], ALU.subtract)
+
+        def duel(t, side):
+            nc.scalar.activation(gate[t][:, side, :], diff[t][:], ACT.Sigmoid, scale=1.0 - 2.0 * side)
+            nc.vector.tensor_tensor(dt_rows[t][:].indirect(pair_lists[side][:]), pair[t][:, side, :], gate[t][:, side, :], ALU.mult)
+
+        def leave_b(t):
+            nc.scalar.activation(b_rows[t][:], b_acc[t][:], ACT.Copy, scale=gm_size[:, t : t + 1])
+
+        def take_larger(t):
+            for u in range(2):
+                nc.scalar.activation(larger[:, t, W * u : W * (u + 1)], b_rows[t][:].indirect(n3_l[:, 16 * u : 16 * (u + 1)]), ACT.Copy)
+            nc.vector.tensor_tensor(larger[:, t, :], larger[:, t, :], b_rows[t][:], ALU.max)
+
+        def round_z(t):
+            nc.scalar.activation(z_rows[:, t, :], dt_rows[t][:], ACT.Copy, scale=gn_t[:, t, :])
+
+        leave_a(0)
+        leave_a(1)
+        fetch(0, 0)
+        fetch(0, 1)
+        nc.vector.tensor_copy(walk_out(w1_grouped[:]), walk_in(w1_raw[:]))
+        w1_q = quantize(w1_grouped, N, "w1")
+        leave_a(2)
+        fetch(1, 0)
+        duel(0, 0)
+        fetch(1, 1)
+        duel(0, 1)
+        leave_b(0)
+        fetch(2, 0)
+        leave_a(3)
+        duel(1, 0)
+        fetch(2, 1)
+        duel(1, 1)
+        take_larger(0)
+        leave_b(1)
+        round_z(0)
+        fetch(3, 0)
+        duel(2, 0)
+        fetch(3, 1)
+        duel(2, 1)
+        take_larger(1)
+        leave_b(2)
+        round_z(1)
+        duel(3, 0)
+        take_larger(2)
+        duel(3, 1)
+        leave_b(3)
+        round_z(2)
+        take_larger(3)
+
+        z2_codes = keep.tile([P, S], U32, name="z2_codes", align_bytes=64)
+        z2_scales = keep.tile([P, S], U8, name="z2_scales", align_bytes=64)
+        z_grouped = keep.tile([P, PACK * S], BF16, name="z_grouped", align_bytes=64)
+
+        def smaller(c0, width):
+            other = keep.tile([P, PACK, width], F32, name="other%d" % c0)
+            for t in range(PACK):
+                nc.scalar.activation(other[:, t, :], b_rows[t][:].indirect(n4_l[:, c0 // 16 : (c0 + width) // 16]), ACT.Copy)
+            if c0 == 0:
+                round_z(PACK - 1)
+                nc.vector.tensor_copy(walk_out(z_grouped[:]), walk_in(z_rows[:]))
+            z2_grouped = keep.tile([P, PACK * width], BF16, name="z2_grouped%d" % c0, align_bytes=64)
+            nc.vector.tensor_tensor(walk_out(z2_grouped[:]), walk_in(larger[:, :, c0 : c0 + width]), walk_in(other[:]), ALU.min)
+            return z2_grouped
+
+        def product(acc, m, cols, z_first):
+            rows = slice(P * m, P * (m + 1))
+            passes = [(w1_q, z_q), (w2_q, (z2_codes, z2_scales))]
+            for n, (w_q, moving) in enumerate(passes if z_first else passes[::-1]):
+                nc.tensor.matmul_mx(
+                    out=acc, lhsT=w_q[0][:, rows].bitcast(FP8X4), lhsT_scale=w_q[1][:, rows],
+                    rhs=moving[0][:, cols].bitcast(FP8X4), rhs_scale=moving[1][:, cols], start=(n == 0), stop=(n == 1),
+                )
+
+        first_parts = []
+        for c, (c0, width) in enumerate(CHUNKS):
+            cols = slice(c0, c0 + width)
+            z2_grouped = smaller(c0, width)
+            if c == 0:
+                z_q = quantize(z_grouped, S, "z")
+            nc.vector.quantize_mx(out=z2_codes[:, cols].bitcast(FP8X4), scales=z2_scales[:, cols], in_=z2_grouped[:])
+            acc = psum.tile([P, width], F32, name="h_first%d" % c, tag="bank%d" % (PACK + c))
+            product(acc[:], 0, cols, True)
+            first_parts.append((acc, cols))
+        for acc, cols in first_parts:
+            nc.scalar.copy(h_rows[0][:, cols], acc[:])
+        for m in range(1, 4):
+            acc = psum.tile([P, S], F32, name="h_acc%d" % m, tag="bank%d" % m)
+            product(acc[:], m, slice(0, S), False)
+            nc.vector.tensor_copy(h_rows[m][:, 0:S], acc[:])
+
+        def finish(m, cols, high, bent):
+            result = ring.tile([P, cols.stop - cols.start], F32, name="result", bufs=4)
+            nc.vector.tensor_tensor(result[:], high[:], bent[:], ALU.mult)
+            nc.sync.dma_start(out[P * m : P * (m + 1), cols], result[:])
+
+        waiting = None
+        for m in range(4):
+            for u, width in enumerate(STEPS[m]):
+                j0 = sum(STEPS[m][:u])
+                members = ring.tile([P, width, 4], F32, name="members")
+                flat = members[:].rearrange("p j e -> p (j e)")
+                for e0 in range(0, 4 * width, PIECE):
+                    first = (4 * j0 + e0) // 16
+                    nc.scalar.activation(flat[:, e0 : e0 + PIECE], h_rows[m][:].indirect(n5_l[:, first : first + PIECE // 16]), ACT.Copy)
+                low2 = ring.tile([P, width, 2], F32, name="low2")
+                high2 = ring.tile([P, width, 2], F32, name="high2")
+                low = ring.tile([P, width], F32, name="low")
+                high = ring.tile([P, width], F32, name="high", bufs=3)
+                gap = ring.tile([P, width], F32, name="gap")
+                bent = ring.tile([P, width], F32, name="bent", bufs=3)
+                nc.vector.tensor_tensor(low2[:], members[:, :, 0:2], members[:, :, 2:4], ALU.min)
+                nc.vector.tensor_tensor(high2[:], members[:, :, 0:2], members[:, :, 2:4], ALU.max)
+                nc.vector.tensor_tensor(low[:], low2[:, :, 0], low2[:, :, 1], ALU.min)
+                nc.vector.tensor_tensor(high[:], high2[:, :, 0], high2[:, :, 1], ALU.max)
+                nc.vector.tensor_tensor(gap[:], h_rows[m][:, j0 : j0 + width], low[:], ALU.subtract)
+                nc.scalar.activation(bent[:], gap[:], ACT.Tanh)
+                if waiting is not None:
+                    finish(*waiting)
+                waiting = (m, slice(j0, j0 + width), high, bent)
+        finish(*waiting)

@@ -20,15 +20,16 @@ PACK = 4
 SPARE = 16
 CHUNKS = ((0, 256), (256, 128), (384, 128))
 PIECE = 512
+DW_AFTER = 1
 STEPS = ((256, 256), (256, 256), (256, 256), (256, 128, 128))
 
 
-def walk_out(ap):
-    return ap.rearrange("p (c i t) -> p c t i", i=4, t=PACK)
+def walk_out(ap, run):
+    return ap.rearrange("p (c i t) -> p c t i", i=run, t=PACK)
 
 
-def walk_in(ap):
-    return ap.rearrange("p t (c i) -> p c t i", i=4)
+def walk_in(ap, run):
+    return ap.rearrange("p t (c i) -> p c t i", i=run)
 
 
 def tile_picked_kjduelminmxgtan_none_p_kernel(
@@ -60,11 +61,11 @@ def tile_picked_kjduelminmxgtan_none_p_kernel(
             queue.dma_start(raw[:], src.rearrange("(p t) n -> p t n", t=PACK))
             return raw
 
-        def quantize(grouped, width, name):
-            codes = keep.tile([P, width], U32, name=name + "_codes", align_bytes=64)
+        def quantize(grouped, width, name, tag=None):
+            codes = keep.tile([P, width], U32, name=name + "_codes", tag=tag or name + "_codes", align_bytes=64)
             scales = keep.tile([P, width], U8, name=name + "_scales", align_bytes=64)
-            nc.vector.quantize_mx(out=codes[:].bitcast(FP8X4), scales=scales[:], in_=grouped[:])
-            return codes, scales
+            nc.vector.quantize_mx(out=codes[:].bitcast(FP8X4), scales=scales[:], in_=grouped)
+            return codes[:], scales[:]
 
         placed = keep.tile([P, 3 * S], U8, name="placed", align_bytes=64)
         nc.gpsimd.memset(placed[:].bitcast(I32), 0)
@@ -72,24 +73,28 @@ def tile_picked_kjduelminmxgtan_none_p_kernel(
         for m in range(4):
             nc.gpsimd.memset(h_rows[m][:, S:], 0.0)
 
-        gm_t = load_rows(gm, "gm_t", "gm_t")
-        ds_rows = load_scales(d_scales, G, "ds_rows", "ds_rows")
-        k1_l = load_list(k1, "k1_l")
+        warm = keep.tile([P, 1], F32, name="warm")
+        nc.scalar.activation(warm[:], h_rows[0][:, S : S + 1], ACT.Sigmoid)
+
         xs_rows = load_scales(x_scales, T, "xs_rows", "xs_rows")
         offs_l = load_list(offs, "offs_l")
         two_l = load_list(two, "two_l")
+        ds_rows = load_scales(d_scales, G, "ds_rows", "ds_rows")
+        k1_l = load_list(k1, "k1_l")
+        gm_t = load_rows(gm, "gm_t", "gm_t")
         xw = load_words(x_words, T, "xw")
         w2_raw = [keep.tile([P, N], F32, name="w2_raw%d" % t) for t in range(PACK)]
         for t in range(PACK):
             nc.sync.dma_start(w2_raw[t][:], w2.rearrange("(p t) n -> p t n", t=PACK)[:, t, :])
-        dw = load_words(d_words, G, "dw")
+            if t == DW_AFTER:
+                dw = load_words(d_words, G, "dw")
         n1_l = load_list(n1, "n1_l")
         n2_l = load_list(n2, "n2_l")
 
         picked = keep.tile([P, 3 * S], U8, name="picked", tag="picked_then_w1")
-        nc.vector.tensor_copy(picked[:, 0:S], ds_rows[:].indirect(k1_l[:]))
         nc.vector.tensor_copy(picked[:, S : 2 * S], xs_rows[:].indirect(offs_l[:]))
         nc.vector.tensor_copy(picked[:, 2 * S : 3 * S], xs_rows[:].indirect(two_l[:]))
+        nc.vector.tensor_copy(picked[:, 0:S], ds_rows[:].indirect(k1_l[:]))
         dealt = keep.tile([P, 3 * S], U8, name="dealt")
         nc.vector.tensor_copy(
             dealt[:, 0:S].rearrange("p (t m) -> p t m", t=PACK),
@@ -111,8 +116,12 @@ def tile_picked_kjduelminmxgtan_none_p_kernel(
         w2_signed = keep.tile([P, PACK, N], BF16, name="w2_signed")
         for t in range(PACK):
             nc.scalar.activation(w2_signed[:, t, :], w2_raw[t][:], ACT.Copy, scale=gm_sign[:, t : t + 1])
-        w2_grouped = keep.tile([P, PACK * N], BF16, name="w2_grouped", align_bytes=64)
-        nc.scalar.copy(walk_out(w2_grouped[:]), walk_in(w2_signed[:]))
+        w2_grouped = [keep.tile([P, PACK * P], BF16, name="w2_grouped%d" % m, align_bytes=64) for m in range(4)]
+
+        def group_w2(m):
+            nc.scalar.copy(walk_out(w2_grouped[m][:], 4), walk_in(w2_signed[:, :, P * m : P * (m + 1)], 4))
+
+        group_w2(0)
 
         xa = keep.tile([P, S], U32, name="xa", align_bytes=64)
         keys = keep.tile([P, H], U32, name="keys", tag="keys_then_xb", align_bytes=64)
@@ -143,7 +152,7 @@ def tile_picked_kjduelminmxgtan_none_p_kernel(
         a_acc = [scores(t, xa, slice(S, 2 * S), "bank%d" % t) for t in range(PACK)]
         b_acc = [scores(t, xb, slice(2 * S, 3 * S), "bank%d" % (PACK + t)) for t in range(PACK)]
 
-        w2_q = quantize(w2_grouped, N, "w2")
+        w2_q = [quantize(w2_grouped[0][:], P, "w2_0")]
         w1_grouped = keep.tile([P, PACK * N], BF16, name="w1_grouped", align_bytes=64)
 
         z_rows = keep.tile([P, PACK, S], BF16, name="z_rows")
@@ -161,7 +170,10 @@ def tile_picked_kjduelminmxgtan_none_p_kernel(
         pair_lists = (n1_l, n2_l)
 
         def fetch(t, side):
-            nc.scalar.activation(pair[t][:, side, :], a_rows[t][:].indirect(pair_lists[side][:]), ACT.Copy)
+            if (t, side) == (0, 1):
+                nc.vector.tensor_copy(pair[t][:, side, :], a_rows[t][:].indirect(pair_lists[side][:]))
+            else:
+                nc.scalar.activation(pair[t][:, side, :], a_rows[t][:].indirect(pair_lists[side][:]), ACT.Copy)
             if side == 1:
                 nc.vector.tensor_tensor(diff[t][:], pair[t][:, 0, :], pair[t][:, 1, :], ALU.subtract)
 
@@ -184,8 +196,8 @@ def tile_picked_kjduelminmxgtan_none_p_kernel(
         leave_a(1)
         fetch(0, 0)
         fetch(0, 1)
-        nc.vector.tensor_copy(walk_out(w1_grouped[:]), walk_in(w1_raw[:]))
-        w1_q = quantize(w1_grouped, N, "w1")
+        nc.vector.tensor_copy(walk_out(w1_grouped[:], 2), walk_in(w1_raw[:], 2))
+        w1_q = [quantize(w1_grouped[:, 0 : PACK * P], P, "w1_0")]
         leave_a(2)
         fetch(1, 0)
         duel(0, 0)
@@ -207,10 +219,10 @@ def tile_picked_kjduelminmxgtan_none_p_kernel(
         take_larger(1)
         leave_b(2)
         round_z(1)
+        leave_b(3)
         duel(3, 0)
         take_larger(2)
         duel(3, 1)
-        leave_b(3)
         round_z(2)
         take_larger(3)
 
@@ -219,22 +231,21 @@ def tile_picked_kjduelminmxgtan_none_p_kernel(
         z_grouped = keep.tile([P, PACK * S], BF16, name="z_grouped", align_bytes=64)
 
         def smaller(c0, width):
-            other = keep.tile([P, PACK, width], F32, name="other%d" % c0)
+            other = keep.tile([P, PACK, width], F32, name="other%d" % c0, align_bytes=64)
             for t in range(PACK):
                 nc.scalar.activation(other[:, t, :], b_rows[t][:].indirect(n4_l[:, c0 // 16 : (c0 + width) // 16]), ACT.Copy)
             if c0 == 0:
                 round_z(PACK - 1)
-                nc.vector.tensor_copy(walk_out(z_grouped[:]), walk_in(z_rows[:]))
+                nc.vector.tensor_copy(walk_out(z_grouped[:], 4), walk_in(z_rows[:], 4))
             z2_grouped = keep.tile([P, PACK * width], BF16, name="z2_grouped%d" % c0, align_bytes=64)
-            nc.vector.tensor_tensor(walk_out(z2_grouped[:]), walk_in(larger[:, :, c0 : c0 + width]), walk_in(other[:]), ALU.min)
+            nc.vector.tensor_tensor(walk_out(z2_grouped[:], 2), walk_in(larger[:, :, c0 : c0 + width], 2), walk_in(other[:], 2), ALU.min)
             return z2_grouped
 
         def product(acc, m, cols, z_first):
-            rows = slice(P * m, P * (m + 1))
-            passes = [(w1_q, z_q), (w2_q, (z2_codes, z2_scales))]
+            passes = [(w1_q[m], z_q), (w2_q[m], (z2_codes, z2_scales))]
             for n, (w_q, moving) in enumerate(passes if z_first else passes[::-1]):
                 nc.tensor.matmul_mx(
-                    out=acc, lhsT=w_q[0][:, rows].bitcast(FP8X4), lhsT_scale=w_q[1][:, rows],
+                    out=acc, lhsT=w_q[0].bitcast(FP8X4), lhsT_scale=w_q[1],
                     rhs=moving[0][:, cols].bitcast(FP8X4), rhs_scale=moving[1][:, cols], start=(n == 0), stop=(n == 1),
                 )
 
@@ -243,45 +254,56 @@ def tile_picked_kjduelminmxgtan_none_p_kernel(
             cols = slice(c0, c0 + width)
             z2_grouped = smaller(c0, width)
             if c == 0:
-                z_q = quantize(z_grouped, S, "z")
+                z_q = quantize(z_grouped[:], S, "z")
             nc.vector.quantize_mx(out=z2_codes[:, cols].bitcast(FP8X4), scales=z2_scales[:, cols], in_=z2_grouped[:])
             acc = psum.tile([P, width], F32, name="h_first%d" % c, tag="bank%d" % (PACK + c))
             product(acc[:], 0, cols, True)
             first_parts.append((acc, cols))
         for acc, cols in first_parts:
             nc.scalar.copy(h_rows[0][:, cols], acc[:])
+        w1_rest = quantize(w1_grouped[:, PACK * P :], 3 * P, "w1_rest", "other384")
         for m in range(1, 4):
+            group_w2(m)
+            w2_q.append(quantize(w2_grouped[m][:], P, "w2_%d" % m))
+            w1_q.append(tuple(part[:, P * (m - 1) : P * m] for part in w1_rest))
+
+        def leave_h(m):
             acc = psum.tile([P, S], F32, name="h_acc%d" % m, tag="bank%d" % m)
             product(acc[:], m, slice(0, S), False)
             nc.vector.tensor_copy(h_rows[m][:, 0:S], acc[:])
+
+        leave_h(1)
+        leave_h(2)
 
         def finish(m, cols, high, bent):
             result = ring.tile([P, cols.stop - cols.start], F32, name="result", bufs=4)
             nc.vector.tensor_tensor(result[:], high[:], bent[:], ALU.mult)
             nc.sync.dma_start(out[P * m : P * (m + 1), cols], result[:])
 
+        fetched = [keep.tile([P, 2 * PIECE], F32, name="fetched%d" % k) for k in range(2)]
+        steps = [(m, sum(STEPS[m][:u]), width) for m in range(4) for u, width in enumerate(STEPS[m])]
         waiting = None
-        for m in range(4):
-            for u, width in enumerate(STEPS[m]):
-                j0 = sum(STEPS[m][:u])
-                members = ring.tile([P, width, 4], F32, name="members")
-                flat = members[:].rearrange("p j e -> p (j e)")
-                for e0 in range(0, 4 * width, PIECE):
-                    first = (4 * j0 + e0) // 16
-                    nc.scalar.activation(flat[:, e0 : e0 + PIECE], h_rows[m][:].indirect(n5_l[:, first : first + PIECE // 16]), ACT.Copy)
-                low2 = ring.tile([P, width, 2], F32, name="low2")
-                high2 = ring.tile([P, width, 2], F32, name="high2")
-                low = ring.tile([P, width], F32, name="low")
-                high = ring.tile([P, width], F32, name="high", bufs=3)
-                gap = ring.tile([P, width], F32, name="gap")
-                bent = ring.tile([P, width], F32, name="bent", bufs=3)
-                nc.vector.tensor_tensor(low2[:], members[:, :, 0:2], members[:, :, 2:4], ALU.min)
-                nc.vector.tensor_tensor(high2[:], members[:, :, 0:2], members[:, :, 2:4], ALU.max)
-                nc.vector.tensor_tensor(low[:], low2[:, :, 0], low2[:, :, 1], ALU.min)
-                nc.vector.tensor_tensor(high[:], high2[:, :, 0], high2[:, :, 1], ALU.max)
-                nc.vector.tensor_tensor(gap[:], h_rows[m][:, j0 : j0 + width], low[:], ALU.subtract)
-                nc.scalar.activation(bent[:], gap[:], ACT.Tanh)
-                if waiting is not None:
-                    finish(*waiting)
-                waiting = (m, slice(j0, j0 + width), high, bent)
+        for k, (m, j0, width) in enumerate(steps):
+            flat = fetched[k % 2]
+            for e0 in range(0, 4 * width, PIECE):
+                first, count = (4 * j0 + e0) // 16, min(PIECE, 4 * width - e0)
+                nc.scalar.activation(flat[:, e0 : e0 + count], h_rows[m][:].indirect(n5_l[:, first : first + count // 16]), ACT.Copy)
+            members = flat[:, 0 : 4 * width].rearrange("p (j e) -> p j e", e=4)
+            low2 = ring.tile([P, width, 2], F32, name="low2")
+            high2 = ring.tile([P, width, 2], F32, name="high2")
+            low = flat[:, 2 * PIECE - width :]
+            high = ring.tile([P, width], F32, name="high", bufs=3)
+            gap = ring.tile([P, width], F32, name="gap")
+            bent = ring.tile([P, width], F32, name="bent", bufs=3)
+            nc.vector.tensor_tensor(high2[:], members[:, :, 0:2], members[:, :, 2:4], ALU.max)
+            nc.vector.tensor_tensor(low2[:], members[:, :, 0:2], members[:, :, 2:4], ALU.min)
+            nc.vector.tensor_tensor(high[:], high2[:, :, 0], high2[:, :, 1], ALU.max)
+            nc.vector.tensor_tensor(low, low2[:, :, 0], low2[:, :, 1], ALU.min)
+            if waiting is not None:
+                finish(*waiting)
+            nc.vector.tensor_tensor(gap[:], h_rows[m][:, j0 : j0 + width], low, ALU.subtract)
+            nc.scalar.activation(bent[:], gap[:], ACT.Tanh)
+            waiting = (m, slice(j0, j0 + width), high, bent)
+            if k == 1:
+                leave_h(3)
         finish(*waiting)

@@ -20,7 +20,6 @@ PACK = 4
 SPARE = 16
 CHUNKS = ((0, 256), (256, 128), (384, 128))
 PIECE = 512
-DW_AFTER = 1
 STEPS = ((256, 256), (256, 256), (256, 256), (256, 128, 128))
 
 
@@ -67,7 +66,7 @@ def tile_picked_kjduelminmxgtan_none_p_kernel(
             nc.vector.quantize_mx(out=codes[:].bitcast(FP8X4), scales=scales[:], in_=grouped)
             return codes[:], scales[:]
 
-        placed = keep.tile([P, 3 * S], U8, name="placed", align_bytes=64)
+        placed = keep.tile([P, H], U8, name="placed", align_bytes=64)
         nc.gpsimd.memset(placed[:].bitcast(I32), 0)
         h_rows = [keep.tile([P, S + SPARE], F32, name="h_rows%d" % m) for m in range(4)]
         for m in range(4):
@@ -76,33 +75,35 @@ def tile_picked_kjduelminmxgtan_none_p_kernel(
         warm = keep.tile([P, 1], F32, name="warm")
         nc.scalar.activation(warm[:], h_rows[0][:, S : S + 1], ACT.Sigmoid)
 
-        xs_rows = load_scales(x_scales, T, "xs_rows", "xs_rows")
+        xs_rows = keep.tile([P, T], U8, name="xs_rows")
+        for q in range(4):
+            rows = x_scales[0].bitcast(I32)[4 * q : 4 * q + 4, :]
+            nc.sync.dma_start(xs_rows[32 * q : 32 * q + 32, :].bitcast(I32), rows.unsqueeze(0).to_broadcast([8, 4, T // 4]))
         offs_l = load_list(offs, "offs_l")
-        two_l = load_list(two, "two_l")
         ds_rows = load_scales(d_scales, G, "ds_rows", "ds_rows")
         k1_l = load_list(k1, "k1_l")
+        dw = load_words(d_words, G, "dw")
         gm_t = load_rows(gm, "gm_t", "gm_t")
-        xw = load_words(x_words, T, "xw")
         w2_raw = [keep.tile([P, N], F32, name="w2_raw%d" % t) for t in range(PACK)]
         for t in range(PACK):
             nc.sync.dma_start(w2_raw[t][:], w2.rearrange("(p t) n -> p t n", t=PACK)[:, t, :])
-            if t == DW_AFTER:
-                dw = load_words(d_words, G, "dw")
-        n1_l = load_list(n1, "n1_l")
-        n2_l = load_list(n2, "n2_l")
+            if t == 0:
+                xw = load_words(x_words, T, "xw")
+                two_l = load_list(two, "two_l")
+                n1_l = load_list(n1, "n1_l")
+                n2_l = load_list(n2, "n2_l")
 
-        picked = keep.tile([P, 3 * S], U8, name="picked", tag="picked_then_w1")
-        nc.vector.tensor_copy(picked[:, S : 2 * S], xs_rows[:].indirect(offs_l[:]))
-        nc.vector.tensor_copy(picked[:, 2 * S : 3 * S], xs_rows[:].indirect(two_l[:]))
-        nc.vector.tensor_copy(picked[:, 0:S], ds_rows[:].indirect(k1_l[:]))
-        dealt = keep.tile([P, 3 * S], U8, name="dealt")
+        picked = keep.tile([P, H], U8, name="picked", tag="picked_then_w1")
+        nc.vector.tensor_copy(picked[:], ds_rows[:].indirect(k1_l[:]))
+        dealt = keep.tile([P, H], U8, name="dealt")
         nc.vector.tensor_copy(
-            dealt[:, 0:S].rearrange("p (t m) -> p t m", t=PACK),
-            picked[:, 0:S].rearrange("p (m t) -> p t m", t=PACK),
+            dealt[:].rearrange("p (t m) -> p t m", t=PACK),
+            picked[:].rearrange("p (m t) -> p t m", t=PACK),
         )
-        nc.vector.tensor_copy(dealt[:, S:].bitcast(I32), picked[:, S:].bitcast(I32))
         for r in range(4):
             nc.sync.dma_start(placed[r:P:32, :].bitcast(I32), dealt[8 * r : P : 32, :].bitcast(I32))
+        xa_scales = keep.tile([P, S], U8, name="xa_scales", align_bytes=64)
+        nc.vector.tensor_copy(xa_scales[:], xs_rows[:].indirect(offs_l[:]))
         w1_raw = load_rows(w1, "w1_raw", "picked_then_w1")
         gn_t = load_rows(gn, "gn_t", "gn_t")
         n3_l = load_list(n3, "n3_l")
@@ -114,28 +115,33 @@ def tile_picked_kjduelminmxgtan_none_p_kernel(
         nc.scalar.activation(gm_sign[:], gm_t[:, :, 0], ACT.Sign)
         nc.scalar.activation(gm_size[:], gm_t[:, :, 0], ACT.Abs, scale=0.0625)
         w2_signed = keep.tile([P, PACK, N], BF16, name="w2_signed")
-        for t in range(PACK):
-            nc.scalar.activation(w2_signed[:, t, :], w2_raw[t][:], ACT.Copy, scale=gm_sign[:, t : t + 1])
-        w2_grouped = [keep.tile([P, PACK * P], BF16, name="w2_grouped%d" % m, align_bytes=64) for m in range(4)]
 
         def group_w2(m):
-            nc.scalar.copy(walk_out(w2_grouped[m][:], 4), walk_in(w2_signed[:, :, P * m : P * (m + 1)], 4))
+            grouped = keep.tile([P, PACK * P], BF16, name="w2_grouped%d" % m, tag="pair%d" % m if m else "w2_grouped0", align_bytes=64)
+            nc.scalar.copy(walk_out(grouped[:], 4), walk_in(w2_signed[:, :, P * m : P * (m + 1)], 4))
+            return quantize(grouped[:], P, "w2_%d" % m)
 
-        group_w2(0)
+        def sign_w2(t):
+            nc.scalar.activation(w2_signed[:, t, :], w2_raw[t][:], ACT.Copy, scale=gm_sign[:, t : t + 1])
+
+        sign_w2(0)
+        sign_w2(1)
 
         xa = keep.tile([P, S], U32, name="xa", align_bytes=64)
         keys = keep.tile([P, H], U32, name="keys", tag="keys_then_xb", align_bytes=64)
-        nc.vector.tensor_copy(xa[:], xw[:].indirect(offs_l[:]))
         nc.vector.tensor_copy(keys[:], dw[:].indirect(k1_l[:]))
         keys_dealt = keep.tile([P, H], U32, name="keys_dealt", align_bytes=64)
         nc.vector.tensor_copy(
             keys_dealt[:].bitcast(I32).rearrange("p (t c i) -> p c t i", t=PACK, i=4),
             keys[:].bitcast(I32).rearrange("p (c i t) -> p c t i", t=PACK, i=4),
         )
+        nc.vector.tensor_copy(xa[:], xw[:].indirect(offs_l[:]))
         xb = keep.tile([P, S], U32, name="xb", tag="keys_then_xb", align_bytes=64)
         nc.vector.tensor_copy(xb[:], xw[:].indirect(two_l[:]))
+        xb_scales = keep.tile([P, S], U8, name="xb_scales", align_bytes=64)
+        nc.vector.tensor_copy(xb_scales[:], xs_rows[:].indirect(two_l[:]))
 
-        def scores(t, words, scale_cols, bank):
+        def scores(t, words, scales, bank):
             acc = psum.tile([P, S], F32, name="acc_" + bank, tag=bank)
             cols = slice(P * t, P * (t + 1))
             nc.tensor.matmul_mx(
@@ -143,24 +149,23 @@ def tile_picked_kjduelminmxgtan_none_p_kernel(
                 lhsT=keys_dealt[:, cols].bitcast(FP8X4),
                 lhsT_scale=placed[:, cols],
                 rhs=words[:].bitcast(FP8X4),
-                rhs_scale=placed[:, scale_cols],
+                rhs_scale=scales[:],
                 start=True,
                 stop=True,
             )
             return acc
 
-        a_acc = [scores(t, xa, slice(S, 2 * S), "bank%d" % t) for t in range(PACK)]
-        b_acc = [scores(t, xb, slice(2 * S, 3 * S), "bank%d" % (PACK + t)) for t in range(PACK)]
+        a_acc = [scores(t, xa, xa_scales, "bank%d" % t) for t in range(PACK)]
+        b_acc = [scores(t, xb, xb_scales, "bank%d" % (PACK + t)) for t in range(PACK)]
 
-        w2_q = [quantize(w2_grouped[0][:], P, "w2_0")]
-        w1_grouped = keep.tile([P, PACK * N], BF16, name="w1_grouped", align_bytes=64)
+        w1_first = keep.tile([P, 2 * PACK * P], BF16, name="w1_first", align_bytes=64)
 
         z_rows = keep.tile([P, PACK, S], BF16, name="z_rows")
         larger = keep.tile([P, PACK, S], F32, name="larger")
         a_rows = [keep.tile([P, S], F32, name="a_rows%d" % t) for t in range(PACK)]
         b_rows = [keep.tile([P, S], F32, name="b_rows%d" % t) for t in range(PACK)]
         dt_rows = [keep.tile([P, S], F32, name="dt_rows%d" % t) for t in range(PACK)]
-        pair = [keep.tile([P, 2, W], F32, name="pair%d" % t) for t in range(PACK)]
+        pair = [keep.tile([P, 2, W], F32, name="pair%d" % t, align_bytes=64) for t in range(PACK)]
         gate = [keep.tile([P, 2, W], F32, name="gate%d" % t) for t in range(PACK)]
         diff = [keep.tile([P, W], F32, name="diff%d" % t) for t in range(PACK)]
 
@@ -196,8 +201,6 @@ def tile_picked_kjduelminmxgtan_none_p_kernel(
         leave_a(1)
         fetch(0, 0)
         fetch(0, 1)
-        nc.vector.tensor_copy(walk_out(w1_grouped[:], 2), walk_in(w1_raw[:], 2))
-        w1_q = [quantize(w1_grouped[:, 0 : PACK * P], P, "w1_0")]
         leave_a(2)
         fetch(1, 0)
         duel(0, 0)
@@ -209,13 +212,18 @@ def tile_picked_kjduelminmxgtan_none_p_kernel(
         duel(1, 0)
         fetch(2, 1)
         duel(1, 1)
+        sign_w2(2)
         take_larger(0)
+        nc.vector.tensor_copy(walk_out(w1_first[:], 2), walk_in(w1_raw[:, :, 0 : 2 * P], 2))
+        w1_early = quantize(w1_first[:], 2 * P, "w1_early")
+        w1_q = [tuple(part[:, P * m : P * (m + 1)] for part in w1_early) for m in range(2)]
         leave_b(1)
         round_z(0)
         fetch(3, 0)
         duel(2, 0)
         fetch(3, 1)
         duel(2, 1)
+        sign_w2(3)
         take_larger(1)
         leave_b(2)
         round_z(1)
@@ -223,6 +231,7 @@ def tile_picked_kjduelminmxgtan_none_p_kernel(
         duel(3, 0)
         take_larger(2)
         duel(3, 1)
+        w2_q = [group_w2(0)]
         round_z(2)
         take_larger(3)
 
@@ -249,6 +258,11 @@ def tile_picked_kjduelminmxgtan_none_p_kernel(
                     rhs=moving[0][:, cols].bitcast(FP8X4), rhs_scale=moving[1][:, cols], start=(n == 0), stop=(n == 1),
                 )
 
+        def leave_h(m):
+            acc = psum.tile([P, S], F32, name="h_acc%d" % m, tag="bank%d" % m)
+            product(acc[:], m, slice(0, S), False)
+            nc.vector.tensor_copy(h_rows[m][:, 0:S], acc[:])
+
         first_parts = []
         for c, (c0, width) in enumerate(CHUNKS):
             cols = slice(c0, c0 + width)
@@ -261,19 +275,14 @@ def tile_picked_kjduelminmxgtan_none_p_kernel(
             first_parts.append((acc, cols))
         for acc, cols in first_parts:
             nc.scalar.copy(h_rows[0][:, cols], acc[:])
-        w1_rest = quantize(w1_grouped[:, PACK * P :], 3 * P, "w1_rest", "other384")
-        for m in range(1, 4):
-            group_w2(m)
-            w2_q.append(quantize(w2_grouped[m][:], P, "w2_%d" % m))
-            w1_q.append(tuple(part[:, P * (m - 1) : P * m] for part in w1_rest))
-
-        def leave_h(m):
-            acc = psum.tile([P, S], F32, name="h_acc%d" % m, tag="bank%d" % m)
-            product(acc[:], m, slice(0, S), False)
-            nc.vector.tensor_copy(h_rows[m][:, 0:S], acc[:])
-
+        w2_q.append(group_w2(1))
         leave_h(1)
-        leave_h(2)
+        w1_grouped = keep.tile([P, 2 * PACK * P], BF16, name="w1_grouped", tag="other384", align_bytes=64)
+        nc.vector.tensor_copy(walk_out(w1_grouped[:], 2), walk_in(w1_raw[:, :, 2 * P :], 2))
+        w1_rest = quantize(w1_grouped[:], 2 * P, "w1_rest")
+        w1_q.extend(tuple(part[:, P * m : P * (m + 1)] for part in w1_rest) for m in range(2))
+        for m in range(2, 4):
+            w2_q.append(group_w2(m))
 
         def finish(m, cols, high, bent):
             result = ring.tile([P, cols.stop - cols.start], F32, name="result", bufs=4)
@@ -301,9 +310,9 @@ def tile_picked_kjduelminmxgtan_none_p_kernel(
             nc.vector.tensor_tensor(low, low2[:, :, 0], low2[:, :, 1], ALU.min)
             if waiting is not None:
                 finish(*waiting)
+            if k in (0, 2):
+                leave_h(2 + k // 2)
             nc.vector.tensor_tensor(gap[:], h_rows[m][:, j0 : j0 + width], low, ALU.subtract)
             nc.scalar.activation(bent[:], gap[:], ACT.Tanh)
             waiting = (m, slice(j0, j0 + width), high, bent)
-            if k == 1:
-                leave_h(3)
         finish(*waiting)

@@ -20,7 +20,7 @@ PACK = 4
 SPARE = 16
 CHUNKS = ((0, 256), (256, 128), (384, 128))
 PIECE = 512
-STEPS = ((256, 256), (256, 256), (256, 256), (256, 128, 128))
+STEPS = ((256, 256), (256, 256), (256, 256), (256, 192, 64))
 
 
 def walk_out(ap, run):
@@ -291,7 +291,7 @@ def tile_picked_kjduelminmxgtan_none_p_kernel(
 
         fetched = [keep.tile([P, 2 * PIECE], F32, name="fetched%d" % k) for k in range(2)]
         steps = [(m, sum(STEPS[m][:u]), width) for m in range(4) for u, width in enumerate(STEPS[m])]
-        waiting = None
+        waiting = []
         for k, (m, j0, width) in enumerate(steps):
             flat = fetched[k % 2]
             for e0 in range(0, 4 * width, PIECE):
@@ -301,18 +301,21 @@ def tile_picked_kjduelminmxgtan_none_p_kernel(
             low2 = ring.tile([P, width, 2], F32, name="low2")
             high2 = ring.tile([P, width, 2], F32, name="high2")
             low = flat[:, 2 * PIECE - width :]
-            high = ring.tile([P, width], F32, name="high", bufs=3)
+            high = ring.tile([P, width], F32, name="high", bufs=4)
             gap = ring.tile([P, width], F32, name="gap")
-            bent = ring.tile([P, width], F32, name="bent", bufs=3)
-            nc.vector.tensor_tensor(high2[:], members[:, :, 0:2], members[:, :, 2:4], ALU.max)
-            nc.vector.tensor_tensor(low2[:], members[:, :, 0:2], members[:, :, 2:4], ALU.min)
+            bent = ring.tile([P, width], F32, name="bent", bufs=4)
+            for c0 in range(0, width, PIECE // 4):
+                part = slice(c0, min(width, c0 + PIECE // 4))
+                nc.vector.tensor_tensor(high2[:, part, :], members[:, part, 0:2], members[:, part, 2:4], ALU.max)
+                nc.vector.tensor_tensor(low2[:, part, :], members[:, part, 0:2], members[:, part, 2:4], ALU.min)
             nc.vector.tensor_tensor(high[:], high2[:, :, 0], high2[:, :, 1], ALU.max)
             nc.vector.tensor_tensor(low, low2[:, :, 0], low2[:, :, 1], ALU.min)
-            if waiting is not None:
-                finish(*waiting)
-            if k in (0, 2):
-                leave_h(2 + k // 2)
+            if len(waiting) == 2:
+                finish(*waiting.pop(0))
+            if k < 2:
+                leave_h(2 + k)
             nc.vector.tensor_tensor(gap[:], h_rows[m][:, j0 : j0 + width], low, ALU.subtract)
             nc.scalar.activation(bent[:], gap[:], ACT.Tanh)
-            waiting = (m, slice(j0, j0 + width), high, bent)
-        finish(*waiting)
+            waiting.append((m, slice(j0, j0 + width), high, bent))
+        for left in waiting:
+            finish(*left)

from contextlib import ExitStack

import concourse.mybir as mybir

K, T, S, N, G, H, W = 512, 1024, 512, 512, 2048, 512, 256
FLOPS = 4 * 2 * 512 * 512 * 512

F32 = mybir.dt.float32
BF16 = mybir.dt.bfloat16
I32 = mybir.dt.int32
U32 = mybir.dt.uint32
U16 = mybir.dt.uint16
U8 = mybir.dt.uint8
FP8X4 = mybir.dt.float8_e4m3fn_x4
ALU = mybir.AluOpType
ACT = mybir.ActivationFunctionType

P = 128
PACK = 4
SPARE = 16
CHUNKS = ((0, 256), (256, 128), (384, 128))
PIECE = 512
STEPS = ((256, 256), (256, 256), (256, 256), (256, 192, 64))


def walk_out(ap, run):
    return ap.rearrange("p (c i t) -> p c t i", i=run, t=PACK)


def walk_in(ap, run):
    return ap.rearrange("p t (c i) -> p c t i", i=run)


def tile_picked_kjduelminmxgtan_none_p_kernel(
    tc, x_words, x_scales, d_words, d_scales, gn, gm, w1, w2, offs, k1, two, n1, n2, n3, n4, n5, out
):
    nc = tc.nc
    with ExitStack() as ctx:
        keep = ctx.enter_context(tc.tile_pool(name="keep", bufs=1))
        ring = ctx.enter_context(tc.tile_pool(name="ring", bufs=2))
        psum = ctx.enter_context(tc.psum_pool(name="psum", bufs=1))

        def load_list(src, name):
            lst = keep.tile(list(src.shape), U16, name=name)
            nc.sync.dma_start(lst[:], src)
            return lst

        def load_scales(src, width, name, tag):
            rows = keep.tile([P, width], U8, name=name, tag=tag)
            nc.sync.dma_start(rows[:].bitcast(I32), src[0].bitcast(I32).unsqueeze(1).to_broadcast([16, 8, width // 4]))
            return rows

        def load_words(src, width, name):
            words = keep.tile([P, width], U32, name=name)
            nc.sync.dma_start(words[:].bitcast(I32), src[0].rearrange("p n t -> p (n t)").bitcast(I32))
            return words

        def load_rows(src, name, tag, queue=nc.sync):
            raw = keep.tile([P, PACK, src.shape[1]], F32, name=name, tag=tag)
            queue.dma_start(raw[:], src.rearrange("(p t) n -> p t n", t=PACK))
            return raw

        def quantize(grouped, width, name, tag=None):
            codes = keep.tile([P, width], U32, name=name + "_codes", tag=tag or name + "_codes", align_bytes=64)
            scales = keep.tile([P, width], U8, name=name + "_scales", align_bytes=64)
            nc.vector.quantize_mx(out=codes[:].bitcast(FP8X4), scales=scales[:], in_=grouped)
            return codes[:], scales[:]

        placed = keep.tile([P, H], U8, name="placed", align_bytes=64)
        nc.gpsimd.memset(placed[:].bitcast(I32), 0)
        h_rows = [keep.tile([P, S + SPARE], F32, name="h_rows%d" % m) for m in range(4)]
        for m in range(4):
            nc.gpsimd.memset(h_rows[m][:, S:], 0.0)

        warm = keep.tile([P, 1], F32, name="warm")
        nc.scalar.activation(warm[:], h_rows[0][:, S : S + 1], ACT.Sigmoid)

        xs_rows = keep.tile([P, T], U8, name="xs_rows")
        for q in range(4):
            rows = x_scales[0].bitcast(I32)[4 * q : 4 * q + 4, :]
            nc.sync.dma_start(xs_rows[32 * q : 32 * q + 32, :].bitcast(I32), rows.unsqueeze(0).to_broadcast([8, 4, T // 4]))
        offs_l = load_list(offs, "offs_l")
        ds_rows = load_scales(d_scales, G, "ds_rows", "ds_rows")
        k1_l = load_list(k1, "k1_l")
        dw = load_words(d_words, G, "dw")
        gm_t = load_rows(gm, "gm_t", "gm_t")
        w2_raw = [keep.tile([P, N], F32, name="w2_raw%d" % t) for t in range(PACK)]
        for t in range(PACK):
            nc.sync.dma_start(w2_raw[t][:], w2.rearrange("(p t) n -> p t n", t=PACK)[:, t, :])
            if t == 0:
                xw = load_words(x_words, T, "xw")
                two_l = load_list(two, "two_l")
                n1_l = load_list(n1, "n1_l")
                n2_l = load_list(n2, "n2_l")

        picked = keep.tile([P, H], U8, name="picked", tag="picked_then_w1")
        nc.vector.tensor_copy(picked[:], ds_rows[:].indirect(k1_l[:]))
        dealt = keep.tile([P, H], U8, name="dealt")
        nc.vector.tensor_copy(
            dealt[:].rearrange("p (t m) -> p t m", t=PACK),
            picked[:].rearrange("p (m t) -> p t m", t=PACK),
        )
        for r in range(4):
            nc.sync.dma_start(placed[r:P:32, :].bitcast(I32), dealt[8 * r : P : 32, :].bitcast(I32))
        xa_scales = keep.tile([P, S], U8, name="xa_scales", align_bytes=64)
        nc.vector.tensor_copy(xa_scales[:], xs_rows[:].indirect(offs_l[:]))
        w1_raw = load_rows(w1, "w1_raw", "picked_then_w1")
        gn_t = load_rows(gn, "gn_t", "gn_t")
        n3_l = load_list(n3, "n3_l")
        n4_l = load_list(n4, "n4_l")
        n5_l = load_list(n5, "n5_l")

        gm_sign = keep.tile([P, PACK], F32, name="gm_sign")
        gm_size = keep.tile([P, PACK], F32, name="gm_size")
        nc.scalar.activation(gm_sign[:], gm_t[:, :, 0], ACT.Sign)
        nc.scalar.activation(gm_size[:], gm_t[:, :, 0], ACT.Abs, scale=0.0625)
        w2_signed = keep.tile([P, PACK, N], BF16, name="w2_signed")

        def group_w2(m):
            grouped = keep.tile([P, PACK * P], BF16, name="w2_grouped%d" % m, tag="pair%d" % m if m else "w2_grouped0", align_bytes=64)
            nc.scalar.copy(walk_out(grouped[:], 4), walk_in(w2_signed[:, :, P * m : P * (m + 1)], 4))
            return quantize(grouped[:], P, "w2_%d" % m)

        def sign_w2(t):
            nc.scalar.activation(w2_signed[:, t, :], w2_raw[t][:], ACT.Copy, scale=gm_sign[:, t : t + 1])

        sign_w2(0)
        sign_w2(1)

        xa = keep.tile([P, S], U32, name="xa", align_bytes=64)
        keys = keep.tile([P, H], U32, name="keys", tag="keys_then_xb", align_bytes=64)
        nc.vector.tensor_copy(keys[:], dw[:].indirect(k1_l[:]))
        keys_dealt = keep.tile([P, H], U32, name="keys_dealt", align_bytes=64)
        nc.vector.tensor_copy(
            keys_dealt[:].bitcast(I32).rearrange("p (t c i) -> p c t i", t=PACK, i=4),
            keys[:].bitcast(I32).rearrange("p (c i t) -> p c t i", t=PACK, i=4),
        )
        nc.vector.tensor_copy(xa[:], xw[:].indirect(offs_l[:]))
        xb = keep.tile([P, S], U32, name="xb", tag="keys_then_xb", align_bytes=64)
        nc.vector.tensor_copy(xb[:], xw[:].indirect(two_l[:]))
        xb_scales = keep.tile([P, S], U8, name="xb_scales", align_bytes=64)
        nc.vector.tensor_copy(xb_scales[:], xs_rows[:].indirect(two_l[:]))

        def scores(t, words, scales, bank):
            acc = psum.tile([P, S], F32, name="acc_" + bank, tag=bank)
            cols = slice(P * t, P * (t + 1))
            nc.tensor.matmul_mx(
                out=acc[:],
                lhsT=keys_dealt[:, cols].bitcast(FP8X4),
                lhsT_scale=placed[:, cols],
                rhs=words[:].bitcast(FP8X4),
                rhs_scale=scales[:],
                start=True,
                stop=True,
            )
            return acc

        a_acc = [scores(t, xa, xa_scales, "bank%d" % t) for t in range(PACK)]
        b_acc = [scores(t, xb, xb_scales, "bank%d" % (PACK + t)) for t in range(PACK)]

        w1_first = keep.tile([P, 2 * PACK * P], BF16, name="w1_first", align_bytes=64)

        z_rows = keep.tile([P, PACK, S], BF16, name="z_rows")
        larger = keep.tile([P, PACK, S], F32, name="larger")
        a_rows = [keep.tile([P, S], F32, name="a_rows%d" % t) for t in range(PACK)]
        b_rows = [keep.tile([P, S], F32, name="b_rows%d" % t) for t in range(PACK)]
        dt_rows = [keep.tile([P, S], F32, name="dt_rows%d" % t) for t in range(PACK)]
        pair = [keep.tile([P, 2, W], F32, name="pair%d" % t, align_bytes=64) for t in range(PACK)]
        gate = [keep.tile([P, 2, W], F32, name="gate%d" % t) for t in range(PACK)]
        diff = [keep.tile([P, W], F32, name="diff%d" % t) for t in range(PACK)]

        def leave_a(t):
            nc.scalar.activation(a_rows[t][:], a_acc[t][:], ACT.Copy, scale=0.0625)

        pair_lists = (n1_l, n2_l)

        def fetch(t, side):
            if (t, side) == (0, 1):
                nc.vector.tensor_copy(pair[t][:, side, :], a_rows[t][:].indirect(pair_lists[side][:]))
            else:
                nc.scalar.activation(pair[t][:, side, :], a_rows[t][:].indirect(pair_lists[side][:]), ACT.Copy)
            if side == 1:
                nc.vector.tensor_tensor(diff[t][:], pair[t][:, 0, :], pair[t][:, 1, :], ALU.subtract)

        def duel(t, side):
            nc.scalar.activation(gate[t][:, side, :], diff[t][:], ACT.Sigmoid, scale=1.0 - 2.0 * side)
            nc.vector.tensor_tensor(dt_rows[t][:].indirect(pair_lists[side][:]), pair[t][:, side, :], gate[t][:, side, :], ALU.mult)

        def leave_b(t):
            nc.scalar.activation(b_rows[t][:], b_acc[t][:], ACT.Copy, scale=gm_size[:, t : t + 1])

        def take_larger(t):
            for u in range(2):
                nc.scalar.activation(larger[:, t, W * u : W * (u + 1)], b_rows[t][:].indirect(n3_l[:, 16 * u : 16 * (u + 1)]), ACT.Copy)
            nc.vector.tensor_tensor(larger[:, t, :], larger[:, t, :], b_rows[t][:], ALU.max)

        def round_z(t):
            nc.scalar.activation(z_rows[:, t, :], dt_rows[t][:], ACT.Copy, scale=gn_t[:, t, :])

        leave_a(0)
        leave_a(1)
        fetch(0, 0)
        fetch(0, 1)
        leave_a(2)
        fetch(1, 0)
        duel(0, 0)
        fetch(1, 1)
        duel(0, 1)
        leave_b(0)
        fetch(2, 0)
        leave_a(3)
        duel(1, 0)
        fetch(2, 1)
        duel(1, 1)
        sign_w2(2)
        take_larger(0)
        nc.vector.tensor_copy(walk_out(w1_first[:], 2), walk_in(w1_raw[:, :, 0 : 2 * P], 2))
        w1_early = quantize(w1_first[:], 2 * P, "w1_early")
        w1_q = [tuple(part[:, P * m : P * (m + 1)] for part in w1_early) for m in range(2)]
        leave_b(1)
        round_z(0)
        fetch(3, 0)
        duel(2, 0)
        fetch(3, 1)
        duel(2, 1)
        sign_w2(3)
        take_larger(1)
        leave_b(2)
        round_z(1)
        leave_b(3)
        duel(3, 0)
        take_larger(2)
        duel(3, 1)
        w2_q = [group_w2(0)]
        round_z(2)
        take_larger(3)

        z2_codes = keep.tile([P, S], U32, name="z2_codes", align_bytes=64)
        z2_scales = keep.tile([P, S], U8, name="z2_scales", align_bytes=64)
        z_grouped = keep.tile([P, PACK * S], BF16, name="z_grouped", align_bytes=64)

        def smaller(c0, width):
            other = keep.tile([P, PACK, width], F32, name="other%d" % c0, align_bytes=64)
            for t in range(PACK):
                nc.scalar.activation(other[:, t, :], b_rows[t][:].indirect(n4_l[:, c0 // 16 : (c0 + width) // 16]), ACT.Copy)
            if c0 == 0:
                round_z(PACK - 1)
                nc.vector.tensor_copy(walk_out(z_grouped[:], 4), walk_in(z_rows[:], 4))
            z2_grouped = keep.tile([P, PACK * width], BF16, name="z2_grouped%d" % c0, align_bytes=64)
            nc.vector.tensor_tensor(walk_out(z2_grouped[:], 2), walk_in(larger[:, :, c0 : c0 + width], 2), walk_in(other[:], 2), ALU.min)
            return z2_grouped

        def product(acc, m, cols, z_first):
            passes = [(w1_q[m], z_q), (w2_q[m], (z2_codes, z2_scales))]
            for n, (w_q, moving) in enumerate(passes if z_first else passes[::-1]):
                nc.tensor.matmul_mx(
                    out=acc, lhsT=w_q[0].bitcast(FP8X4), lhsT_scale=w_q[1],
                    rhs=moving[0][:, cols].bitcast(FP8X4), rhs_scale=moving[1][:, cols], start=(n == 0), stop=(n == 1),
                )

        def leave_h(m):
            acc = psum.tile([P, S], F32, name="h_acc%d" % m, tag="bank%d" % m)
            product(acc[:], m, slice(0, S), False)
            nc.vector.tensor_copy(h_rows[m][:, 0:S], acc[:])

        first_parts = []
        for c, (c0, width) in enumerate(CHUNKS):
            cols = slice(c0, c0 + width)
            z2_grouped = smaller(c0, width)
            if c == 0:
                z_q = quantize(z_grouped[:], S, "z")
            nc.vector.quantize_mx(out=z2_codes[:, cols].bitcast(FP8X4), scales=z2_scales[:, cols], in_=z2_grouped[:])
            acc = psum.tile([P, width], F32, name="h_first%d" % c, tag="bank%d" % (PACK + c))
            product(acc[:], 0, cols, True)
            first_parts.append((acc, cols))
        for acc, cols in first_parts:
            nc.scalar.copy(h_rows[0][:, cols], acc[:])
        w2_q.append(group_w2(1))
        leave_h(1)
        w1_grouped = keep.tile([P, 2 * PACK * P], BF16, name="w1_grouped", tag="other384", align_bytes=64)
        nc.vector.tensor_copy(walk_out(w1_grouped[:], 2), walk_in(w1_raw[:, :, 2 * P :], 2))
        w1_rest = quantize(w1_grouped[:], 2 * P, "w1_rest")
        w1_q.extend(tuple(part[:, P * m : P * (m + 1)] for part in w1_rest) for m in range(2))
        for m in range(2, 4):
            w2_q.append(group_w2(m))

        def finish(m, cols, high, bent):
            result = ring.tile([P, cols.stop - cols.start], F32, name="result", bufs=4)
            nc.vector.tensor_tensor(result[:], high[:], bent[:], ALU.mult)
            nc.sync.dma_start(out[P * m : P * (m + 1), cols], result[:])

        fetched = [keep.tile([P, 2 * PIECE], F32, name="fetched%d" % k) for k in range(2)]
        steps = [(m, sum(STEPS[m][:u]), width) for m in range(4) for u, width in enumerate(STEPS[m])]
        waiting = []
        for k, (m, j0, width) in enumerate(steps):
            flat = fetched[k % 2]
            for e0 in range(0, 4 * width, PIECE):
                first, count = (4 * j0 + e0) // 16, min(PIECE, 4 * width - e0)
                nc.scalar.activation(flat[:, e0 : e0 + count], h_rows[m][:].indirect(n5_l[:, first : first + count // 16]), ACT.Copy)
            members = flat[:, 0 : 4 * width].rearrange("p (j e) -> p j e", e=4)
            low2 = ring.tile([P, width, 2], F32, name="low2")
            high2 = ring.tile([P, width, 2], F32, name="high2")
            low = flat[:, 2 * PIECE - width :]
            high = ring.tile([P, width], F32, name="high", bufs=4)
            gap = ring.tile([P, width], F32, name="gap")
            bent = ring.tile([P, width], F32, name="bent", bufs=4)
            for c0 in range(0, width, PIECE // 4):
                part = slice(c0, min(width, c0 + PIECE // 4))
                nc.vector.tensor_tensor(high2[:, part, :], members[:, part, 0:2], members[:, part, 2:4], ALU.max)
                nc.vector.tensor_tensor(low2[:, part, :], members[:, part, 0:2], members[:, part, 2:4], ALU.min)
            nc.vector.tensor_tensor(high[:], high2[:, :, 0], high2[:, :, 1], ALU.max)
            nc.vector.tensor_tensor(low, low2[:, :, 0], low2[:, :, 1], ALU.min)
            if len(waiting) == 2:
                finish(*waiting.pop(0))
            if k < 2:
                leave_h(2 + k)
            nc.vector.tensor_tensor(gap[:], h_rows[m][:, j0 : j0 + width], low, ALU.subtract)
            nc.scalar.activation(bent[:], gap[:], ACT.Tanh)
            waiting.append((m, slice(j0, j0 + width), high, bent))
        for left in waiting:
            finish(*left)
